import numpy as np
import ml_dtypes


def mxq(x, axis, fmt="e4m3"):
    dtype, down = {"e4m3": (ml_dtypes.float8_e4m3fn, 7), "e5m2": (ml_dtypes.float8_e5m2, 14)}[fmt]
    v = np.moveaxis(np.asarray(x, np.float32).astype(ml_dtypes.bfloat16).astype(np.float64), axis, -1)
    blocks = v.reshape(v.shape[:-1] + (-1, 32))
    amax = np.abs(blocks).max(-1, keepdims=True)
    byte = np.maximum(np.where(amax > 0, np.frexp(amax)[1] - 1 + 127, 0) - down, 1)
    scale = np.exp2(byte - 127.0)
    codes = (blocks / scale).astype(np.float32).astype(dtype).astype(np.float64)
    return np.moveaxis((codes * scale).reshape(v.shape), -1, axis)


WIDE = False


def mx_kscale(k, group=512):
    if not WIDE:
        return np.ones(k)
    levels = np.array([10, -10, 5, -5, 0])
    if group != 512:
        return np.exp2(np.random.permutation(np.resize(levels, k // group))).repeat(group)
    if k % 512:
        return np.exp2(np.random.permutation(np.resize(levels, k // 32))).repeat(32)
    a = np.empty((k // 512, 16))
    for p in range(k // 512):
        a[p, :8] = np.random.permutation(np.resize(levels, 8))
        for g in range(8):
            far = levels[np.abs(levels - a[p, g]) >= 10]
            a[p, g + 8] = far[np.random.randint(len(far))]
    return np.exp2(a.ravel()).repeat(32)


def f64(x):
    return np.asarray(x).astype(np.float64)


E2M1 = np.array([0.0, 0.5, 1.0, 1.5, 2.0, 3.0, 4.0, 6.0, -0.0, -0.5, -1.0, -1.5, -2.0, -3.0, -4.0, -6.0])


def pack_group(w):
    k, n = w.shape
    w = f64(np.asarray(w, np.float32).astype(ml_dtypes.bfloat16)).reshape(k // 32, 32, n)
    amax = np.abs(w).max(1)
    mant, ex = np.frexp(amax / 6.0)
    byte = np.clip(np.where(amax > 0, np.where(mant > 0.5, ex, ex - 1) + 127, 1), 1, 254)
    scaled = (w * np.exp2(127.0 - byte)[:, None, :]).reshape(k, n).astype(np.float32)
    c = np.ascontiguousarray(scaled.reshape(k // 4, 4, n).transpose(0, 2, 1)).astype(ml_dtypes.float4_e2m1fn).view(np.uint8) & 0xF
    return np.ascontiguousarray((c[..., 0::2] | (c[..., 1::2] << 4)).reshape(k // 4, 2 * n)), byte.astype(np.uint8)


def unpack_group(words, scales):
    p, n = words.shape[0], scales.shape[1]
    words = np.ascontiguousarray(words).reshape(p, n, 2)
    nib = np.empty((p, n, 4), np.uint8)
    nib[..., 0::2] = words & 0xF
    nib[..., 1::2] = words >> 4
    return E2M1[nib].transpose(0, 2, 1).reshape(4 * p, n) * np.repeat(np.exp2(scales.astype(np.float64) - 127.0), 32, axis=0)


G, D, M, N = 4, 256, 128, 512


def setup_inputs():
    n = np.random.standard_normal
    s = mx_kscale(D, 0)[:, None]
    w_ = [pack_group(w) for w in n((G, D, M)) / np.sqrt(D) / s]
    return {
        "x": (n((G, D, N)) * s).astype(np.float32),
        "w_words": np.stack([w[0] for w in w_]),
        "w_scales": np.stack([w[1] for w in w_]),
        "b": (0.5 * n((G, M, 1))).astype(np.float32),
        "r": n((G, M, N)).astype(np.float32),
    }


def reference(x, w_words, w_scales, b, r):
    xq = mxq(f64(x), 1, "e4m3")
    y = np.stack([unpack_group(w_words[g], w_scales[g]) for g in range(G)]).transpose(0, 2, 1) @ xq
    y = y + f64(b)
    y = np.square(np.maximum(y, 0.0))
    y = y + f64(r)
    return y

@@ -1,0 +1,135 @@
+from contextlib import ExitStack
+
+import concourse.mybir as mybir
+
+G, D, M, N = 4, 256, 128, 512
+FLOPS = 2 * G * D * M * N
+
+F32 = mybir.dt.float32
+BF16 = mybir.dt.bfloat16
+I32 = mybir.dt.int32
+U32 = mybir.dt.uint32
+U8 = mybir.dt.uint8
+FP8X4 = mybir.dt.float8_e4m3fn_x4
+FP4X4 = mybir.dt.float4_e2m1fn_x4
+ACT = mybir.ActivationFunctionType
+ALU = mybir.AluOpType
+
+P = 128
+PACK = 4
+ROWS = D // PACK
+SIDE = P // ROWS
+PAIRS = G // SIDE
+QUAD = 32
+CHUNK = 256
+HALF = CHUNK // 2
+PAD = N - CHUNK
+
+
+def tile_rows_glin_relu2_bias_res_kernel(tc, x, w_words, w_scales, b, r, out):
+    nc = tc.nc
+    chunks = [(a, c0) for a in range(PAIRS) for c0 in range(0, N, CHUNK)]
+    x_v = x.rearrange("(a c) (p j) n -> a (c p) j n", c=SIDE, j=PACK)
+    r_v = r.rearrange("(a c) m n -> a m c n", c=SIDE)
+    out_v = out.rearrange("(a c) m n -> a m c n", c=SIDE)
+
+    with ExitStack() as ctx:
+        keep = ctx.enter_context(tc.tile_pool(name="keep", bufs=1))
+        psum = ctx.enter_context(tc.psum_pool(name="psum", bufs=1))
+        ctx.enter_context(tc.manual_schedule())
+
+        words = keep.tile([P, PAIRS, 2 * M], U8, align_bytes=64)
+        w_plane = keep.tile([P, PAIRS, M], U8, align_bytes=64)
+        bias_rows = keep.tile([P, G * QUAD], F32, align_bytes=64)
+        bias_cols = keep.tile([P, G * QUAD], F32, align_bytes=64)
+        warm_in = keep.tile([P, 1], F32)
+        warm_out = keep.tile([P, 1], F32)
+        codes = keep.tile([P, PAD + PAIRS * N], U32, align_bytes=64)
+        x_plane = keep.tile([P, PAD + PAIRS * N], U8, align_bytes=64)
+
+        nc.vector.memset(w_plane[:].rearrange("p a m -> p (a m)").bitcast(I32), 0)
+        nc.vector.memset(warm_in[:], 0.0)
+        nc.vector.memset(bias_rows[:], 0.0)
+        nc.vector.memset(codes[:, 0:PAD], 0)
+        nc.vector.memset(x_plane[:, 0:PAD].bitcast(I32), 0)
+
+        scale_rows = w_scales.bitcast(I32).rearrange("(a c) (h i) m -> i (c h) a m", c=SIDE, i=4)
+        for i in range(4):
+            nc.scalar.dma_start(out=w_plane[i:P:QUAD, :, :].bitcast(I32), in_=scale_rows[i])
+
+        nc.scalar.dma_start(
+            out=words[:].bitcast(I32),
+            in_=w_words.bitcast(I32).rearrange("(a c) p n -> (c p) a n", c=SIDE),
+        )
+        nc.scalar.activation(out=warm_out[:], in_=warm_in[:], func=ACT.Square)
+
+        raw = []
+        for k, (a, c0) in enumerate(chunks):
+            t = keep.tile([P, PACK, CHUNK], F32, name="raw%d" % k)
+            nc.sync.dma_start(out=t[:], in_=x_v[a, :, :, c0 : c0 + CHUNK])
+            raw.append(t)
+
+        nc.gpsimd.dma_start(
+            out=bias_rows[0:P:QUAD, :].rearrange("q (g s) -> q g s", g=G),
+            in_=b.rearrange("g (q s) o -> q g (s o)", s=QUAD),
+        )
+
+        res = [keep.tile([P, SIDE, N], F32, name="res%d" % a) for a in range(PAIRS)]
+        sq = [keep.tile([P, SIDE, N], F32, name="sq%d" % a) for a in range(PAIRS)]
+        fin = [keep.tile([P, SIDE, N], F32, name="fin%d" % a) for a in range(PAIRS)]
+        pieces = [(0, slice(0, 1), slice(0, N)), (0, slice(1, 2), slice(0, N))]
+        pieces += [(1, slice(0, SIDE), slice(c0, c0 + CHUNK)) for c0 in range(0, N, CHUNK)]
+        for a, cs, ns in pieces:
+            nc.sync.dma_start(out=res[a][:, cs, ns], in_=r_v[a, :, cs, ns])
+
+        for k, (a, c0) in enumerate(chunks):
+            grouped = keep.tile([P, CHUNK * PACK], BF16, name="grouped%d" % k, align_bytes=64)
+            for h in range(2):
+                nc.vector.tensor_copy(
+                    out=grouped[:, h * HALF * PACK : (h + 1) * HALF * PACK].rearrange(
+                        "p (c i t) -> p c t i", i=4, t=PACK
+                    ),
+                    in_=raw[k][:, :, h * HALF : (h + 1) * HALF].rearrange("p t (c i) -> p c t i", i=4),
+                )
+            start = PAD + a * N + c0
+            for h in range(2):
+                cols = slice(start + h * HALF, start + (h + 1) * HALF)
+                nc.vector.quantize_mx(
+                    out=codes[:, cols].bitcast(FP8X4),
+                    scales=x_plane[:, cols],
+                    in_=grouped[:, h * HALF * PACK : (h + 1) * HALF * PACK],
+                )
+            if k == 0:
+                nc.vector.transpose(out=bias_cols[:], in_=bias_rows[:])
+
+            window = slice(start + CHUNK - N, start + CHUNK)
+            banks = []
+            for c in range(SIDE):
+                rows = slice(c * ROWS, (c + 1) * ROWS)
+                acc = psum.tile([M, N], F32, name="acc%d_%d" % (k, c))
+                nc.tensor.matmul_mx(
+                    out=acc[:],
+                    lhsT=words[rows, a, :].bitcast(FP4X4),
+                    lhsT_scale=w_plane[rows, a, :],
+                    rhs=codes[rows, window].bitcast(FP8X4),
+                    rhs_scale=x_plane[rows, window],
+                    start=True,
+                    stop=True,
+                )
+                banks.append(acc)
+
+            pos = keep.tile([P, SIDE, CHUNK], F32, name="pos%d" % k)
+            for c in range(SIDE):
+                g = a * SIDE + c
+                nc.scalar.activation(
+                    out=pos[:, c, :],
+                    in_=banks[c][:, N - CHUNK : N],
+                    func=ACT.Relu,
+                    bias=bias_cols[:, g * QUAD : g * QUAD + 1],
+                )
+            for c in range(SIDE):
+                nc.scalar.activation(out=sq[a][:, c, c0 : c0 + CHUNK], in_=pos[:, c, :], func=ACT.Square)
+
+        for a, cs, ns in pieces:
+            nc.vector.tensor_tensor(out=fin[a][:, cs, ns], in0=sq[a][:, cs, ns], in1=res[a][:, cs, ns], op=ALU.add)
+            nc.sync.dma_start(out=out_v[a, :, cs, ns], in_=fin[a][:, cs, ns])

@@ -24,6 +24,8 @@ QUAD = 32
 CHUNK = 256
 HALF = CHUNK // 2
 PAD = N - CHUNK
+LOAD_COLS = (256, 256, 128, 128)
+SCALAR_COLS = (64, 64, 0, 0)
 
 
 def tile_rows_glin_relu2_bias_res_kernel(tc, x, w_words, w_scales, b, r, out):
@@ -48,48 +50,58 @@ def tile_rows_glin_relu2_bias_res_kernel(tc, x, w_words, w_scales, b, r, out):
         x_plane = keep.tile([P, PAD + PAIRS * N], U8, align_bytes=64)
 
         nc.vector.memset(w_plane[:].rearrange("p a m -> p (a m)").bitcast(I32), 0)
-        nc.vector.memset(warm_in[:], 0.0)
         nc.vector.memset(bias_rows[:], 0.0)
+        nc.vector.memset(warm_in[:], 0.0)
         nc.vector.memset(codes[:, 0:PAD], 0)
         nc.vector.memset(x_plane[:, 0:PAD].bitcast(I32), 0)
+        nc.scalar.activation(out=warm_out[:], in_=warm_in[:], func=ACT.Square)
 
-        scale_rows = w_scales.bitcast(I32).rearrange("(a c) (h i) m -> i (c h) a m", c=SIDE, i=4)
-        for i in range(4):
-            nc.scalar.dma_start(out=w_plane[i:P:QUAD, :, :].bitcast(I32), in_=scale_rows[i])
-
-        nc.scalar.dma_start(
+        nc.sync.dma_start(
             out=words[:].bitcast(I32),
             in_=w_words.bitcast(I32).rearrange("(a c) p n -> (c p) a n", c=SIDE),
         )
-        nc.scalar.activation(out=warm_out[:], in_=warm_in[:], func=ACT.Square)
-
-        raw = []
+        scale_rows = w_scales.bitcast(I32).rearrange("(a c) (h i) m -> i (c h) a m", c=SIDE, i=4)
+        raw = {}
         for k, (a, c0) in enumerate(chunks):
-            t = keep.tile([P, PACK, CHUNK], F32, name="raw%d" % k)
-            nc.sync.dma_start(out=t[:], in_=x_v[a, :, :, c0 : c0 + CHUNK])
-            raw.append(t)
+            for s0 in range(0, CHUNK, LOAD_COLS[k]):
+                t = keep.tile([P, PACK, LOAD_COLS[k]], F32, name="raw%d_%d" % (k, s0))
+                nc.sync.dma_start(out=t[:], in_=x_v[a, :, :, c0 + s0 : c0 + s0 + LOAD_COLS[k]])
+                raw[k, s0] = t
+            if k == 0:
+                for i in range(4):
+                    nc.sync.dma_start(out=w_plane[i:P:QUAD, :, :].bitcast(I32), in_=scale_rows[i])
+                nc.sync.dma_start(
+                    out=bias_rows[0:P:QUAD, :].rearrange("q (g s) -> q g s", g=G),
+                    in_=b.rearrange("g (q s) o -> q g (s o)", s=QUAD),
+                )
 
-        nc.gpsimd.dma_start(
-            out=bias_rows[0:P:QUAD, :].rearrange("q (g s) -> q g s", g=G),
-            in_=b.rearrange("g (q s) o -> q g (s o)", s=QUAD),
-        )
+        loads = [(0, 0, 1, 0, 512), (0, 1, 1, 0, 512), (1, 0, 2, 0, 256), (1, 0, 2, 256, 256)]
+        stores = [(0, 0, 1, 0, 512), (0, 1, 1, 0, 512), (1, 0, 2, 0, 256), (1, 0, 1, 256, 256), (1, 1, 1, 256, 256)]
+        res, sq = {}, {}
+        for piece in loads:
+            a, g0, gn, n0, nn = piece
+            res[piece] = keep.tile([P, gn, nn], F32, name="res%d_%d_%d" % (a, g0, n0))
+            sq[piece] = keep.tile([P, gn, nn], F32, name="sq%d_%d_%d" % (a, g0, n0))
+            nc.sync.dma_start(out=res[piece][:], in_=r_v[a, :, g0 : g0 + gn, n0 : n0 + nn])
 
-        res = [keep.tile([P, SIDE, N], F32, name="res%d" % a) for a in range(PAIRS)]
-        sq = [keep.tile([P, SIDE, N], F32, name="sq%d" % a) for a in range(PAIRS)]
-        fin = [keep.tile([P, SIDE, N], F32, name="fin%d" % a) for a in range(PAIRS)]
-        pieces = [(0, slice(0, 1), slice(0, N)), (0, slice(1, 2), slice(0, N))]
-        pieces += [(1, slice(0, SIDE), slice(c0, c0 + CHUNK)) for c0 in range(0, N, CHUNK)]
-        for a, cs, ns in pieces:
-            nc.sync.dma_start(out=res[a][:, cs, ns], in_=r_v[a, :, cs, ns])
+        def view(tiles, a, g0, gn, n0, nn):
+            for (ta, tg, tgn, tn, tnn), t in tiles.items():
+                if ta == a and tg <= g0 and g0 + gn <= tg + tgn and tn <= n0 and n0 + nn <= tn + tnn:
+                    return t[:, g0 - tg : g0 - tg + gn, n0 - tn : n0 - tn + nn]
+            raise ValueError("no tile holds this piece")
 
-        for k, (a, c0) in enumerate(chunks):
+        def quantise(k):
+            a, c0 = chunks[k]
             grouped = keep.tile([P, CHUNK * PACK], BF16, name="grouped%d" % k, align_bytes=64)
-            for h in range(2):
-                nc.vector.tensor_copy(
-                    out=grouped[:, h * HALF * PACK : (h + 1) * HALF * PACK].rearrange(
-                        "p (c i t) -> p c t i", i=4, t=PACK
-                    ),
-                    in_=raw[k][:, :, h * HALF : (h + 1) * HALF].rearrange("p t (c i) -> p c t i", i=4),
+            vector_end = CHUNK - SCALAR_COLS[k]
+            shares = [(nc.vector.tensor_copy, 0, HALF), (nc.vector.tensor_copy, HALF, vector_end)]
+            if vector_end < CHUNK:
+                shares.append((nc.scalar.copy, vector_end, CHUNK))
+            for copy, lo, hi in shares:
+                s0 = lo // LOAD_COLS[k] * LOAD_COLS[k]
+                copy(
+                    out=grouped[:, lo * PACK : hi * PACK].rearrange("p (c i t) -> p c t i", i=4, t=PACK),
+                    in_=raw[k, s0][:, :, lo - s0 : hi - s0].rearrange("p t (c i) -> p c t i", i=4),
                 )
             start = PAD + a * N + c0
             for h in range(2):
@@ -99,16 +111,18 @@ def tile_rows_glin_relu2_bias_res_kernel(tc, x, w_words, w_scales, b, r, out):
                     scales=x_plane[:, cols],
                     in_=grouped[:, h * HALF * PACK : (h + 1) * HALF * PACK],
                 )
-            if k == 0:
-                nc.vector.transpose(out=bias_cols[:], in_=bias_rows[:])
 
-            window = slice(start + CHUNK - N, start + CHUNK)
-            banks = []
+        banks = {}
+
+        def multiply(k):
+            a, c0 = chunks[k]
+            end = PAD + a * N + c0 + CHUNK
+            window = slice(end - N, end)
             for c in range(SIDE):
                 rows = slice(c * ROWS, (c + 1) * ROWS)
-                acc = psum.tile([M, N], F32, name="acc%d_%d" % (k, c))
+                banks[k, c] = psum.tile([M, N], F32, name="acc%d_%d" % (k, c))
                 nc.tensor.matmul_mx(
-                    out=acc[:],
+                    out=banks[k, c][:],
                     lhsT=words[rows, a, :].bitcast(FP4X4),
                     lhsT_scale=w_plane[rows, a, :],
                     rhs=codes[rows, window].bitcast(FP8X4),
@@ -116,20 +130,33 @@ def tile_rows_glin_relu2_bias_res_kernel(tc, x, w_words, w_scales, b, r, out):
                     start=True,
                     stop=True,
                 )
-                banks.append(acc)
 
+        def activate(k):
+            a, c0 = chunks[k]
             pos = keep.tile([P, SIDE, CHUNK], F32, name="pos%d" % k)
             for c in range(SIDE):
                 g = a * SIDE + c
                 nc.scalar.activation(
                     out=pos[:, c, :],
-                    in_=banks[c][:, N - CHUNK : N],
+                    in_=banks[k, c][:, N - CHUNK : N],
                     func=ACT.Relu,
                     bias=bias_cols[:, g * QUAD : g * QUAD + 1],
                 )
             for c in range(SIDE):
-                nc.scalar.activation(out=sq[a][:, c, c0 : c0 + CHUNK], in_=pos[:, c, :], func=ACT.Square)
+                nc.scalar.activation(out=view(sq, a, c, 1, c0, CHUNK), in_=pos[:, c : c + 1, :], func=ACT.Square)
 
-        for a, cs, ns in pieces:
-            nc.vector.tensor_tensor(out=fin[a][:, cs, ns], in0=sq[a][:, cs, ns], in1=res[a][:, cs, ns], op=ALU.add)
-            nc.sync.dma_start(out=out_v[a, :, cs, ns], in_=fin[a][:, cs, ns])
+        quantise(0)
+        nc.vector.transpose(out=bias_cols[:], in_=bias_rows[:])
+        multiply(0)
+        for k in range(1, len(chunks)):
+            quantise(k)
+            activate(k - 1)
+            multiply(k)
+        activate(len(chunks) - 1)
+
+        for a, g0, gn, n0, nn in stores:
+            fin = keep.tile([P, gn, nn], F32, name="fin%d_%d_%d" % (a, g0, n0))
+            nc.vector.tensor_tensor(
+                out=fin[:], in0=view(sq, a, g0, gn, n0, nn), in1=view(res, a, g0, gn, n0, nn), op=ALU.add
+            )
+            nc.sync.dma_start(out=out_v[a, :, g0 : g0 + gn, n0 : n0 + nn], in_=fin[:])

@@ -24,8 +24,8 @@ QUAD = 32
 CHUNK = 256
 HALF = CHUNK // 2
 PAD = N - CHUNK
-LOAD_COLS = (256, 256, 128, 128)
-SCALAR_COLS = (64, 64, 0, 0)
+LOAD_COLS = (256, 256, 256, 256)
+SCALAR_COLS = (64, 64, 64, 64)
 
 
 def tile_rows_glin_relu2_bias_res_kernel(tc, x, w_words, w_scales, b, r, out):
@@ -131,28 +131,40 @@ def tile_rows_glin_relu2_bias_res_kernel(tc, x, w_words, w_scales, b, r, out):
                     stop=True,
                 )
 
-        def activate(k):
-            a, c0 = chunks[k]
-            pos = keep.tile([P, SIDE, CHUNK], F32, name="pos%d" % k)
-            for c in range(SIDE):
-                g = a * SIDE + c
-                nc.scalar.activation(
-                    out=pos[:, c, :],
-                    in_=banks[k, c][:, N - CHUNK : N],
-                    func=ACT.Relu,
-                    bias=bias_cols[:, g * QUAD : g * QUAD + 1],
-                )
-            for c in range(SIDE):
-                nc.scalar.activation(out=view(sq, a, c, 1, c0, CHUNK), in_=pos[:, c : c + 1, :], func=ACT.Square)
+        pos = [keep.tile([P, SIDE, CHUNK], F32, name="pos%d" % k) for k in range(len(chunks))]
 
-        quantise(0)
-        nc.vector.transpose(out=bias_cols[:], in_=bias_rows[:])
-        multiply(0)
-        for k in range(1, len(chunks)):
+        def rectify(k, c, on_vector):
+            g = chunks[k][0] * SIDE + c
+            sums = banks[k, c][:, N - CHUNK : N]
+            bias = bias_cols[:, g * QUAD : g * QUAD + 1]
+            if on_vector:
+                nc.vector.tensor_scalar(
+                    out=pos[k][:, c, :], in0=sums, scalar1=bias, scalar2=0.0, op0=ALU.add, op1=ALU.max
+                )
+            else:
+                nc.scalar.activation(out=pos[k][:, c, :], in_=sums, func=ACT.Relu, bias=bias)
+
+        def square(k):
+            a, c0 = chunks[k]
+            for c in range(SIDE):
+                nc.scalar.activation(out=view(sq, a, c, 1, c0, CHUNK), in_=pos[k][:, c : c + 1, :], func=ACT.Square)
+
+        last = len(chunks) - 1
+        for k in range(len(chunks)):
             quantise(k)
-            activate(k - 1)
+            if k == 0:
+                nc.vector.transpose(out=bias_cols[:], in_=bias_rows[:])
+            if k >= 2:
+                rectify(k - 2, 1, False)
+                square(k - 2)
+            if k >= 1:
+                rectify(k - 1, 0, True)
             multiply(k)
-        activate(len(chunks) - 1)
+        rectify(last - 1, 1, False)
+        square(last - 1)
+        rectify(last, 0, False)
+        rectify(last, 1, False)
+        square(last)
 
         for a, g0, gn, n0, nn in stores:
             fin = keep.tile([P, gn, nn], F32, name="fin%d_%d_%d" % (a, g0, n0))

from contextlib import ExitStack

import concourse.mybir as mybir

G, D, M, N = 4, 256, 128, 512
FLOPS = 2 * G * D * M * N

F32 = mybir.dt.float32
BF16 = mybir.dt.bfloat16
I32 = mybir.dt.int32
U32 = mybir.dt.uint32
U8 = mybir.dt.uint8
FP8X4 = mybir.dt.float8_e4m3fn_x4
FP4X4 = mybir.dt.float4_e2m1fn_x4
ACT = mybir.ActivationFunctionType
ALU = mybir.AluOpType

P = 128
PACK = 4
ROWS = D // PACK
SIDE = P // ROWS
PAIRS = G // SIDE
QUAD = 32
CHUNK = 256
HALF = CHUNK // 2
PAD = N - CHUNK
LOAD_COLS = (256, 256, 256, 256)
SCALAR_COLS = (64, 64, 64, 64)


def tile_rows_glin_relu2_bias_res_kernel(tc, x, w_words, w_scales, b, r, out):
    nc = tc.nc
    chunks = [(a, c0) for a in range(PAIRS) for c0 in range(0, N, CHUNK)]
    x_v = x.rearrange("(a c) (p j) n -> a (c p) j n", c=SIDE, j=PACK)
    r_v = r.rearrange("(a c) m n -> a m c n", c=SIDE)
    out_v = out.rearrange("(a c) m n -> a m c n", c=SIDE)

    with ExitStack() as ctx:
        keep = ctx.enter_context(tc.tile_pool(name="keep", bufs=1))
        psum = ctx.enter_context(tc.psum_pool(name="psum", bufs=1))
        ctx.enter_context(tc.manual_schedule())

        words = keep.tile([P, PAIRS, 2 * M], U8, align_bytes=64)
        w_plane = keep.tile([P, PAIRS, M], U8, align_bytes=64)
        bias_rows = keep.tile([P, G * QUAD], F32, align_bytes=64)
        bias_cols = keep.tile([P, G * QUAD], F32, align_bytes=64)
        warm_in = keep.tile([P, 1], F32)
        warm_out = keep.tile([P, 1], F32)
        codes = keep.tile([P, PAD + PAIRS * N], U32, align_bytes=64)
        x_plane = keep.tile([P, PAD + PAIRS * N], U8, align_bytes=64)

        nc.vector.memset(w_plane[:].rearrange("p a m -> p (a m)").bitcast(I32), 0)
        nc.vector.memset(bias_rows[:], 0.0)
        nc.vector.memset(warm_in[:], 0.0)
        nc.vector.memset(codes[:, 0:PAD], 0)
        nc.vector.memset(x_plane[:, 0:PAD].bitcast(I32), 0)
        nc.scalar.activation(out=warm_out[:], in_=warm_in[:], func=ACT.Square)

        nc.sync.dma_start(
            out=words[:].bitcast(I32),
            in_=w_words.bitcast(I32).rearrange("(a c) p n -> (c p) a n", c=SIDE),
        )
        scale_rows = w_scales.bitcast(I32).rearrange("(a c) (h i) m -> i (c h) a m", c=SIDE, i=4)
        raw = {}
        for k, (a, c0) in enumerate(chunks):
            for s0 in range(0, CHUNK, LOAD_COLS[k]):
                t = keep.tile([P, PACK, LOAD_COLS[k]], F32, name="raw%d_%d" % (k, s0))
                nc.sync.dma_start(out=t[:], in_=x_v[a, :, :, c0 + s0 : c0 + s0 + LOAD_COLS[k]])
                raw[k, s0] = t
            if k == 0:
                for i in range(4):
                    nc.sync.dma_start(out=w_plane[i:P:QUAD, :, :].bitcast(I32), in_=scale_rows[i])
                nc.sync.dma_start(
                    out=bias_rows[0:P:QUAD, :].rearrange("q (g s) -> q g s", g=G),
                    in_=b.rearrange("g (q s) o -> q g (s o)", s=QUAD),
                )

        loads = [(0, 0, 1, 0, 512), (0, 1, 1, 0, 512), (1, 0, 2, 0, 256), (1, 0, 2, 256, 256)]
        stores = [(0, 0, 1, 0, 512), (0, 1, 1, 0, 512), (1, 0, 2, 0, 256), (1, 0, 1, 256, 256), (1, 1, 1, 256, 256)]
        res, sq = {}, {}
        for piece in loads:
            a, g0, gn, n0, nn = piece
            res[piece] = keep.tile([P, gn, nn], F32, name="res%d_%d_%d" % (a, g0, n0))
            sq[piece] = keep.tile([P, gn, nn], F32, name="sq%d_%d_%d" % (a, g0, n0))
            nc.sync.dma_start(out=res[piece][:], in_=r_v[a, :, g0 : g0 + gn, n0 : n0 + nn])

        def view(tiles, a, g0, gn, n0, nn):
            for (ta, tg, tgn, tn, tnn), t in tiles.items():
                if ta == a and tg <= g0 and g0 + gn <= tg + tgn and tn <= n0 and n0 + nn <= tn + tnn:
                    return t[:, g0 - tg : g0 - tg + gn, n0 - tn : n0 - tn + nn]
            raise ValueError("no tile holds this piece")

        def quantise(k):
            a, c0 = chunks[k]
            grouped = keep.tile([P, CHUNK * PACK], BF16, name="grouped%d" % k, align_bytes=64)
            vector_end = CHUNK - SCALAR_COLS[k]
            shares = [(nc.vector.tensor_copy, 0, HALF), (nc.vector.tensor_copy, HALF, vector_end)]
            if vector_end < CHUNK:
                shares.append((nc.scalar.copy, vector_end, CHUNK))
            for copy, lo, hi in shares:
                s0 = lo // LOAD_COLS[k] * LOAD_COLS[k]
                copy(
                    out=grouped[:, lo * PACK : hi * PACK].rearrange("p (c i t) -> p c t i", i=4, t=PACK),
                    in_=raw[k, s0][:, :, lo - s0 : hi - s0].rearrange("p t (c i) -> p c t i", i=4),
                )
            start = PAD + a * N + c0
            for h in range(2):
                cols = slice(start + h * HALF, start + (h + 1) * HALF)
                nc.vector.quantize_mx(
                    out=codes[:, cols].bitcast(FP8X4),
                    scales=x_plane[:, cols],
                    in_=grouped[:, h * HALF * PACK : (h + 1) * HALF * PACK],
                )

        banks = {}

        def multiply(k):
            a, c0 = chunks[k]
            end = PAD + a * N + c0 + CHUNK
            window = slice(end - N, end)
            for c in range(SIDE):
                rows = slice(c * ROWS, (c + 1) * ROWS)
                banks[k, c] = psum.tile([M, N], F32, name="acc%d_%d" % (k, c))
                nc.tensor.matmul_mx(
                    out=banks[k, c][:],
                    lhsT=words[rows, a, :].bitcast(FP4X4),
                    lhsT_scale=w_plane[rows, a, :],
                    rhs=codes[rows, window].bitcast(FP8X4),
                    rhs_scale=x_plane[rows, window],
                    start=True,
                    stop=True,
                )

        pos = [keep.tile([P, SIDE, CHUNK], F32, name="pos%d" % k) for k in range(len(chunks))]

        def rectify(k, c, on_vector):
            g = chunks[k][0] * SIDE + c
            sums = banks[k, c][:, N - CHUNK : N]
            bias = bias_cols[:, g * QUAD : g * QUAD + 1]
            if on_vector:
                nc.vector.tensor_scalar(
                    out=pos[k][:, c, :], in0=sums, scalar1=bias, scalar2=0.0, op0=ALU.add, op1=ALU.max
                )
            else:
                nc.scalar.activation(out=pos[k][:, c, :], in_=sums, func=ACT.Relu, bias=bias)

        def square(k):
            a, c0 = chunks[k]
            for c in range(SIDE):
                nc.scalar.activation(out=view(sq, a, c, 1, c0, CHUNK), in_=pos[k][:, c : c + 1, :], func=ACT.Square)

        last = len(chunks) - 1
        for k in range(len(chunks)):
            quantise(k)
            if k == 0:
                nc.vector.transpose(out=bias_cols[:], in_=bias_rows[:])
            if k >= 2:
                rectify(k - 2, 1, False)
                square(k - 2)
            if k >= 1:
                rectify(k - 1, 0, True)
            multiply(k)
        rectify(last - 1, 1, False)
        square(last - 1)
        rectify(last, 0, False)
        rectify(last, 1, False)
        square(last)

        for a, g0, gn, n0, nn in stores:
            fin = keep.tile([P, gn, nn], F32, name="fin%d_%d_%d" % (a, g0, n0))
            nc.vector.tensor_tensor(
                out=fin[:], in0=view(sq, a, g0, gn, n0, nn), in1=view(res, a, g0, gn, n0, nn), op=ALU.add
            )
            nc.sync.dma_start(out=out_v[a, :, g0 : g0 + gn, n0 : n0 + nn], in_=fin[:])
